import numpy as np, ml_dtypes
CORES = [5,13,21,29,133,141,149,157,261,389]
N = 10
ROOT = 8
def setup_inputs(rng):
    return {"x": rng.standard_normal((N, 128, 8), dtype=np.float32).astype(ml_dtypes.bfloat16)}
def reference(x):
    y = np.full(x.shape, np.nan, x.dtype)
    y[ROOT] = x.min(axis=0)
    return {"y": y}

from concourse.bass import DstId, RemoteDMATransfer

SCRATCH = {
    "mine": ("dram", [128, 8], "bfloat16"),
    "land": ("dram", [5, 128, 8], "bfloat16"),
}
SEMAPHORES = ["loaded", "arrived", "sent", "result", "stored"]

ENGINES = 0x0F
NENG = 4
MIN = 3


def rank_program(g, core, T, topo):
    cores = list(T.cores)
    root = cores[T.root]
    fold = cores[4]
    odd = cores[5] + 2
    far = cores[9]

    rack0 = [c for c in cores if topo.rack(topo.host(c)) == 0]
    to_fold = [c for c in rack0 if topo.chip(c) % 2 == 0 and c != fold]
    to_odd = [c for c in rack0 if topo.chip(c) % 2 == 1]
    ODD_SLOT, RACK1_SLOT = len(to_fold), len(to_fold) + 1
    FAR_SLOT, RESULT_SLOT = 0, 1

    def send(dst, slot, srcs, sem):
        rid, pid = topo.addr(dst, core)
        if len(srcs) == 1:
            g.remote_dma(T.land[slot], srcs[0], sem, T.sem.sent, pid, rid, ENGINES)
        else:
            g.remote_dma_fused(
                [RemoteDMATransfer(dst_ids=[DstId(rid=rid, pnc=pid)], dma_engine_mask=ENGINES, remote_sem=sem,
                                   srcs=srcs, dsts=[T.land[slot]], alu_op=MIN)],
                local_sem=T.sem.sent)
        g.wait_ge(T.sem.sent, NENG)

    if core == odd:
        g.wait_ge(T.sem.arrived, NENG * len(to_odd))
        send(fold, ODD_SLOT, [T.land[k] for k in range(len(to_odd))], T.sem.arrived)
        return
    if T.rank_of(core) is None:
        return

    g.sync.dma_start(T.mine[:], T.x[:]).then_inc(T.sem.loaded, 16)
    g.wait_ge(T.sem.loaded, 16)

    if core in to_fold:
        send(fold, to_fold.index(core), [T.mine[:]], T.sem.arrived)
    elif core in to_odd:
        send(odd, to_odd.index(core), [T.mine[:]], T.sem.arrived)
    elif core == far:
        send(root, FAR_SLOT, [T.mine[:]], T.sem.arrived)
    elif core == fold:
        g.wait_ge(T.sem.arrived, NENG * (len(to_fold) + 2))
        send(root, RESULT_SLOT, [T.mine[:]] + [T.land[k] for k in range(len(to_fold) + 2)], T.sem.result)
    elif core == root:
        g.wait_ge(T.sem.arrived, NENG)
        send(fold, RACK1_SLOT, [T.mine[:], T.land[FAR_SLOT]], T.sem.arrived)
        g.sync.wait_ge(T.sem.result, NENG)
        g.sync.dma_start(T.y[:], T.land[RESULT_SLOT]).then_inc(T.sem.stored, 16)
        g.sync.wait_ge(T.sem.stored, 16)
